import numpy as np
import ml_dtypes


def mxq(x, axis, fmt="e4m3"):
    dtype, down = {"e4m3": (ml_dtypes.float8_e4m3fn, 7), "e5m2": (ml_dtypes.float8_e5m2, 14)}[fmt]
    v = np.moveaxis(np.asarray(x, np.float32).astype(ml_dtypes.bfloat16).astype(np.float64), axis, -1)
    blocks = v.reshape(v.shape[:-1] + (-1, 32))
    amax = np.abs(blocks).max(-1, keepdims=True)
    byte = np.maximum(np.where(amax > 0, np.frexp(amax)[1] - 1 + 127, 0) - down, 1)
    scale = np.exp2(byte - 127.0)
    codes = (blocks / scale).astype(np.float32).astype(dtype).astype(np.float64)
    return np.moveaxis((codes * scale).reshape(v.shape), -1, axis)


WIDE = False


def mx_kscale(k):
    if not WIDE:
        return np.ones(k)
    levels = np.array([10, -10, 5, -5, 0])
    if k % 512:
        return np.exp2(np.random.permutation(np.resize(levels, k // 32))).repeat(32)
    a = np.empty((k // 512, 16))
    for p in range(k // 512):
        a[p, :8] = np.random.permutation(np.resize(levels, 8))
        for g in range(8):
            far = levels[np.abs(levels - a[p, g]) >= 10]
            a[p, g + 8] = far[np.random.randint(len(far))]
    return np.exp2(a.ravel()).repeat(32)


def f64(x):
    return np.asarray(x).astype(np.float64)


def striped8(idx):
    return np.asarray(idx).reshape(8, -1, 16).transpose(0, 2, 1).reshape(128, -1).astype(np.uint16)


def unstriped8(offs):
    return offs.reshape(8, 16, -1).transpose(0, 2, 1).reshape(8, -1).astype(np.int64)


def pick8(x, idx, run):
    r = np.arange(len(x))
    return x[r[:, None], idx[r % (8 * run) // run]]


E2M1 = np.array([0.0, 0.5, 1.0, 1.5, 2.0, 3.0, 4.0, 6.0, -0.0, -0.5, -1.0, -1.5, -2.0, -3.0, -4.0, -6.0])


def pack_weight(w, fmt):
    k, n = w.shape
    w = f64(np.asarray(w, np.float32).astype(ml_dtypes.bfloat16)).reshape(k // 32, 32, n)
    amax = np.abs(w).max(1)
    if fmt == "e4m3":
        byte = np.frexp(amax)[1] - 1 + 127 - 7
    else:
        mant, ex = np.frexp(amax / 6.0)
        byte = np.where(mant > 0.5, ex, ex - 1) + 127
    byte = np.clip(np.where(amax > 0, byte, 1), 1, 254)
    scaled = (w * np.exp2(127.0 - byte)[:, None, :]).reshape(k, n).astype(np.float32)
    by_word = np.ascontiguousarray(scaled.reshape(k // 512, 128, 4, n).transpose(0, 1, 3, 2))
    if fmt == "e4m3":
        words = by_word.astype(ml_dtypes.float8_e4m3fn).view(np.uint8)
    else:
        c = by_word.astype(ml_dtypes.float4_e2m1fn).view(np.uint8) & 0xF
        words = (c[..., 0::2] | (c[..., 1::2] << 4)).reshape(k // 512, 128, 2 * n)
    return np.ascontiguousarray(words), np.ascontiguousarray(byte.astype(np.uint8).reshape(k // 512, 16, n))


def unpack_weight(words, scales, fmt):
    g, _, n = scales.shape
    words = np.ascontiguousarray(words).reshape(g, 128, n, -1)
    if fmt == "e4m3":
        vals = words.view(ml_dtypes.float8_e4m3fn).astype(np.float64)
    else:
        nib = np.empty((g, 128, n, 4), np.uint8)
        nib[..., 0::2] = words & 0xF
        nib[..., 1::2] = words >> 4
        vals = E2M1[nib]
    vals = vals * np.repeat(np.exp2(scales.astype(np.float64) - 127.0), 8, axis=1)[..., None]
    return vals.transpose(0, 1, 3, 2).reshape(g * 512, n)


K, T, J, N = 512, 1024, 512, 512


def setup_inputs():
    n = np.random.standard_normal
    idx = np.stack([np.random.permutation(T)[:J] for _ in range(8)])
    idx2 = np.stack([np.random.permutation(T)[:J] for _ in range(8)])
    fk = mx_kscale(K)
    xtp = pack_weight(n((K, T)) / fk[:, None], "e4m3")
    wbp = pack_weight(n((K, N)) * 1 / np.sqrt(K) * fk[:, None], "e2m1")
    return {
        "xt_words": xtp[0],
        "xt_scales": xtp[1],
        "wa": (n((K, N)) * 1 / np.sqrt(K) * fk[:, None]).astype(np.float32),
        "wb_words": wbp[0],
        "wb_scales": wbp[1],
        "offs": striped8(idx),
        "offs2": striped8(idx2),
    }


def reference(xt_words, xt_scales, wa, wb_words, wb_scales, offs, offs2):
    idx = unstriped8(offs)
    idx2 = unstriped8(offs2)
    xtu = unpack_weight(xt_words, xt_scales, "e4m3")
    wbu = unpack_weight(wb_words, wb_scales, "e2m1")
    waq = mxq(f64(wa), 0, "e4m3")
    xtidxg = pick8(xtu, idx, 64)
    p = waq.T @ xtidxg
    xtidx2g = pick8(xtu, idx2, 64)
    q = wbu.T @ xtidx2g
    y = np.maximum(p, q) - 0.3 * np.minimum(p, q)
    return y

@@ -1,0 +1,126 @@
+from contextlib import ExitStack
+
+import concourse.mybir as mybir
+
+K, T, J, N = 512, 1024, 512, 512
+FLOPS = 2 * 2 * K * N * J
+
+F32 = mybir.dt.float32
+BF16 = mybir.dt.bfloat16
+I32 = mybir.dt.int32
+U32 = mybir.dt.uint32
+U16 = mybir.dt.uint16
+U8 = mybir.dt.uint8
+FP8X4 = mybir.dt.float8_e4m3fn_x4
+FP4X4 = mybir.dt.float4_e2m1fn_x4
+ALU = mybir.AluOpType
+
+P = 128
+PACK = 4
+TILES = N // P
+HALF = J // 2
+
+
+def tile_moe_expert_heads_twice_kernel(tc, xt_words, xt_scales, wa, wb_words, wb_scales, offs, offs2, out):
+    nc = tc.nc
+    with ExitStack() as ctx:
+        keep = ctx.enter_context(tc.tile_pool(name="keep", bufs=1))
+        psum = ctx.enter_context(tc.psum_pool(name="psum", bufs=1))
+
+        list_a = keep.tile([P, J // 16], U16, name="list_a")
+        list_b = keep.tile([P, J // 16], U16, name="list_b")
+        scale_window = keep.tile([P, T], U8, name="scale_window", align_bytes=64)
+        word_window = keep.tile([P, T], I32, name="word_window", align_bytes=64)
+        picked_scales = keep.tile([P, 2 * J], U8, name="picked_scales", align_bytes=64)
+        x_plane = keep.tile([P, 2 * J], U8, name="x_plane", align_bytes=64)
+        wb_plane = keep.tile([P, N], U8, name="wb_plane", align_bytes=64)
+        wb_codes = keep.tile([P, 2 * N], U8, name="wb_codes", align_bytes=64)
+        xa = keep.tile([P, J], U32, name="xa", align_bytes=64)
+        xb = keep.tile([P, J], U32, name="xb", align_bytes=64)
+
+        nc.sync.dma_start(list_b[:], offs2)
+        nc.sync.dma_start(list_a[:], offs)
+        nc.sync.dma_start(
+            scale_window[:].bitcast(I32), xt_scales[0].bitcast(I32).unsqueeze(1).to_broadcast([16, 8, T // 4])
+        )
+        nc.sync.dma_start(word_window[:], xt_words[0].rearrange("p c r -> p (c r)").bitcast(I32))
+        nc.sync.dma_start(wb_codes[:].bitcast(I32), wb_words[0].bitcast(I32))
+        wa_rows = wa.rearrange("(p r) n -> p r n", r=PACK)
+        wa_raw = []
+        for h in range(2):
+            raw = keep.tile([P, PACK, N // 2], F32, name="wa_raw%d" % h)
+            nc.sync.dma_start(raw[:], wa_rows[:, :, h * (N // 2) : (h + 1) * (N // 2)])
+            wa_raw.append(raw)
+        for x in range(4):
+            nc.scalar.dma_start(
+                wb_plane[32 * x : 32 * x + 32, :].bitcast(I32),
+                wb_scales[0][4 * x : 4 * x + 4, :].bitcast(I32).unsqueeze(0).to_broadcast([8, 4, N // 4]),
+            )
+        nc.vector.memset(x_plane[:].bitcast(I32), 0)
+
+        nc.vector.tensor_copy(picked_scales[:, J : 2 * J], scale_window[:].indirect(list_b[:]))
+        nc.vector.tensor_copy(picked_scales[:, 0:J], scale_window[:].indirect(list_a[:]))
+        for x in range(4):
+            nc.sync.dma_start(
+                x_plane[32 * x : 32 * x + 4, :].bitcast(I32), picked_scales[32 * x : 32 * x + 32 : 8, :].bitcast(I32)
+            )
+        nc.vector.tensor_copy(xb[:], word_window[:].bitcast(U32).indirect(list_b[:]))
+        nc.vector.tensor_copy(xa[:], word_window[:].bitcast(U32).indirect(list_a[:]))
+
+        grouped = []
+
+        def cast(m):
+            g = keep.tile([P, P, PACK], BF16, name="wa_grouped%d" % m, align_bytes=64)
+            raw = wa_raw[m // 2]
+            c0 = (m % 2) * P
+            nc.scalar.copy(g[:], raw[:, :, c0 : c0 + P].rearrange("p r n -> p n r"))
+            grouped.append(g)
+
+        cast(0)
+        cast(1)
+        halves = [slice(h * HALF, (h + 1) * HALF) for h in range(2)]
+        for m in range(TILES):
+            q_bank = psum.tile([P, J], F32, name="q_bank%d" % m)
+            nc.tensor.matmul_mx(
+                out=q_bank[:],
+                lhsT=wb_codes[:, 2 * m * P : 2 * (m + 1) * P].bitcast(FP4X4),
+                lhsT_scale=wb_plane[:, m * P : (m + 1) * P],
+                rhs=xb[:].bitcast(FP8X4),
+                rhs_scale=x_plane[:, J : 2 * J],
+                start=True,
+                stop=True,
+            )
+            q_copy = keep.tile([P, J], F32, name="q_copy%d" % m)
+            nc.scalar.copy(q_copy[:], q_bank[:])
+            if m + 2 < TILES:
+                cast(m + 2)
+
+            codes = keep.tile([P, P], U32, name="wa_codes%d" % m, align_bytes=64)
+            plane = keep.tile([P, P], U8, name="wa_plane%d" % m, align_bytes=64)
+            nc.vector.quantize_mx(
+                out=codes[:].bitcast(FP8X4), scales=plane[:], in_=grouped[m][:].rearrange("p n r -> p (n r)")
+            )
+            p_bank = psum.tile([P, J], F32, name="p_bank%d" % m)
+            nc.tensor.matmul_mx(
+                out=p_bank[:],
+                lhsT=codes[:].bitcast(FP8X4),
+                lhsT_scale=plane[:],
+                rhs=xa[:].bitcast(FP8X4),
+                rhs_scale=x_plane[:, 0:J],
+                start=True,
+                stop=True,
+            )
+
+            low = keep.tile([P, J], F32, name="low%d" % m)
+            part = keep.tile([P, J], F32, name="part%d" % m)
+            result = keep.tile([P, J], F32, name="result%d" % m)
+            for cols in halves:
+                nc.vector.tensor_tensor(low[:, cols], p_bank[:, cols], q_copy[:, cols], ALU.min)
+            for cols in halves:
+                nc.vector.scalar_tensor_tensor(part[:, cols], low[:, cols], -1.3, p_bank[:, cols], ALU.mult, ALU.add)
+            for cols in halves:
+                if m < TILES - 1:
+                    nc.gpsimd.tensor_tensor(result[:, cols], part[:, cols], q_copy[:, cols], ALU.add)
+                else:
+                    nc.vector.tensor_tensor(result[:, cols], q_bank[:, cols], part[:, cols], ALU.add)
+            nc.sync.dma_start(out[m * P : (m + 1) * P, :], result[:])

@@ -31,96 +31,153 @@ def tile_moe_expert_heads_twice_kernel(tc, xt_words, xt_scales, wa, wb_words, wb
         list_b = keep.tile([P, J // 16], U16, name="list_b")
         scale_window = keep.tile([P, T], U8, name="scale_window", align_bytes=64)
         word_window = keep.tile([P, T], I32, name="word_window", align_bytes=64)
-        picked_scales = keep.tile([P, 2 * J], U8, name="picked_scales", align_bytes=64)
-        x_plane = keep.tile([P, 2 * J], U8, name="x_plane", align_bytes=64)
         wb_plane = keep.tile([P, N], U8, name="wb_plane", align_bytes=64)
         wb_codes = keep.tile([P, 2 * N], U8, name="wb_codes", align_bytes=64)
-        xa = keep.tile([P, J], U32, name="xa", align_bytes=64)
-        xb = keep.tile([P, J], U32, name="xb", align_bytes=64)
-
-        nc.sync.dma_start(list_b[:], offs2)
-        nc.sync.dma_start(list_a[:], offs)
-        nc.sync.dma_start(
-            scale_window[:].bitcast(I32), xt_scales[0].bitcast(I32).unsqueeze(1).to_broadcast([16, 8, T // 4])
-        )
-        nc.sync.dma_start(word_window[:], xt_words[0].rearrange("p c r -> p (c r)").bitcast(I32))
-        nc.sync.dma_start(wb_codes[:].bitcast(I32), wb_words[0].bitcast(I32))
+        wa_raw = [keep.tile([P, PACK, N // 2], F32, name="wa_raw%d" % h) for h in range(2)]
         wa_rows = wa.rearrange("(p r) n -> p r n", r=PACK)
-        wa_raw = []
-        for h in range(2):
-            raw = keep.tile([P, PACK, N // 2], F32, name="wa_raw%d" % h)
-            nc.sync.dma_start(raw[:], wa_rows[:, :, h * (N // 2) : (h + 1) * (N // 2)])
-            wa_raw.append(raw)
-        for x in range(4):
-            nc.scalar.dma_start(
+
+        def load_wb_scales(x):
+            nc.sync.dma_start(
                 wb_plane[32 * x : 32 * x + 32, :].bitcast(I32),
                 wb_scales[0][4 * x : 4 * x + 4, :].bitcast(I32).unsqueeze(0).to_broadcast([8, 4, N // 4]),
             )
-        nc.vector.memset(x_plane[:].bitcast(I32), 0)
 
-        nc.vector.tensor_copy(picked_scales[:, J : 2 * J], scale_window[:].indirect(list_b[:]))
-        nc.vector.tensor_copy(picked_scales[:, 0:J], scale_window[:].indirect(list_a[:]))
-        for x in range(4):
-            nc.sync.dma_start(
-                x_plane[32 * x : 32 * x + 4, :].bitcast(I32), picked_scales[32 * x : 32 * x + 32 : 8, :].bitcast(I32)
-            )
-        nc.vector.tensor_copy(xb[:], word_window[:].bitcast(U32).indirect(list_b[:]))
-        nc.vector.tensor_copy(xa[:], word_window[:].bitcast(U32).indirect(list_a[:]))
+        nc.sync.dma_start(
+            scale_window[:].bitcast(I32), xt_scales[0].bitcast(I32).unsqueeze(1).to_broadcast([16, 8, T // 4])
+        )
+        nc.sync.dma_start(list_b[:], offs2)
+        nc.sync.dma_start(list_a[:], offs)
+        nc.sync.dma_start(wa_raw[0][:], wa_rows[:, :, 0 : N // 2])
+        for x in range(3):
+            load_wb_scales(x)
+        nc.sync.dma_start(word_window[:], xt_words[0].rearrange("p c r -> p (c r)").bitcast(I32))
+        load_wb_scales(3)
+        nc.sync.dma_start(wb_codes[:].bitcast(I32), wb_words[0].bitcast(I32))
+        nc.sync.dma_start(wa_raw[1][:], wa_rows[:, :, N // 2 : N])
 
-        grouped = []
+        x_planes = []
+        for h in range(2):
+            entries = slice(h * HALF // 16, (h + 1) * HALF // 16)
+            x_plane = keep.tile([P, 2 * HALF], U8, name="x_plane%d" % h, align_bytes=64)
+            nc.vector.memset(x_plane[:].bitcast(I32), 0)
+            picked = keep.tile([P, 2 * HALF], U8, name="picked_scales%d" % h, align_bytes=64)
+            nc.vector.tensor_copy(picked[:, HALF : 2 * HALF], scale_window[:].indirect(list_b[:, entries]))
+            nc.vector.tensor_copy(picked[:, 0:HALF], scale_window[:].indirect(list_a[:, entries]))
+            for x in range(4):
+                nc.sync.dma_start(
+                    x_plane[32 * x : 32 * x + 4, :].bitcast(I32), picked[32 * x : 32 * x + 32 : 8, :].bitcast(I32)
+                )
+            x_planes.append(x_plane)
+
+        wa_codes, wa_planes, grouped, xa, xb = [], [], [], [], []
 
         def cast(m):
             g = keep.tile([P, P, PACK], BF16, name="wa_grouped%d" % m, align_bytes=64)
-            raw = wa_raw[m // 2]
             c0 = (m % 2) * P
-            nc.scalar.copy(g[:], raw[:, :, c0 : c0 + P].rearrange("p r n -> p n r"))
+            nc.scalar.copy(g[:], wa_raw[m // 2][:, :, c0 : c0 + P].rearrange("p r n -> p n r"))
             grouped.append(g)
 
-        cast(0)
-        cast(1)
-        halves = [slice(h * HALF, (h + 1) * HALF) for h in range(2)]
-        for m in range(TILES):
-            q_bank = psum.tile([P, J], F32, name="q_bank%d" % m)
-            nc.tensor.matmul_mx(
-                out=q_bank[:],
-                lhsT=wb_codes[:, 2 * m * P : 2 * (m + 1) * P].bitcast(FP4X4),
-                lhsT_scale=wb_plane[:, m * P : (m + 1) * P],
-                rhs=xb[:].bitcast(FP8X4),
-                rhs_scale=x_plane[:, J : 2 * J],
-                start=True,
-                stop=True,
-            )
-            q_copy = keep.tile([P, J], F32, name="q_copy%d" % m)
-            nc.scalar.copy(q_copy[:], q_bank[:])
-            if m + 2 < TILES:
-                cast(m + 2)
-
+        def quantize(m):
             codes = keep.tile([P, P], U32, name="wa_codes%d" % m, align_bytes=64)
             plane = keep.tile([P, P], U8, name="wa_plane%d" % m, align_bytes=64)
             nc.vector.quantize_mx(
                 out=codes[:].bitcast(FP8X4), scales=plane[:], in_=grouped[m][:].rearrange("p n r -> p (n r)")
             )
-            p_bank = psum.tile([P, J], F32, name="p_bank%d" % m)
-            nc.tensor.matmul_mx(
-                out=p_bank[:],
-                lhsT=codes[:].bitcast(FP8X4),
-                lhsT_scale=plane[:],
-                rhs=xa[:].bitcast(FP8X4),
-                rhs_scale=x_plane[:, 0:J],
-                start=True,
-                stop=True,
-            )
+            wa_codes.append(codes)
+            wa_planes.append(plane)
 
-            low = keep.tile([P, J], F32, name="low%d" % m)
-            part = keep.tile([P, J], F32, name="part%d" % m)
-            result = keep.tile([P, J], F32, name="result%d" % m)
-            for cols in halves:
-                nc.vector.tensor_tensor(low[:, cols], p_bank[:, cols], q_copy[:, cols], ALU.min)
-            for cols in halves:
-                nc.vector.scalar_tensor_tensor(part[:, cols], low[:, cols], -1.3, p_bank[:, cols], ALU.mult, ALU.add)
-            for cols in halves:
-                if m < TILES - 1:
-                    nc.gpsimd.tensor_tensor(result[:, cols], part[:, cols], q_copy[:, cols], ALU.add)
+        def gather_words(h):
+            entries = slice(h * HALF // 16, (h + 1) * HALF // 16)
+            for name, offsets, picked in (("xb", list_b, xb), ("xa", list_a, xa)):
+                words = keep.tile([P, HALF], U32, name="%s%d" % (name, h), align_bytes=64)
+                nc.vector.tensor_copy(words[:], word_window[:].bitcast(U32).indirect(offsets[:, entries]))
+                picked.append(words)
+
+        cast(0)
+        cast(1)
+        gather_words(0)
+        quantize(0)
+        quantize(1)
+        gather_words(1)
+        cast(2)
+
+        for h in range(2):
+            cols = slice(h * HALF, (h + 1) * HALF)
+            for pair in range(2):
+                step = 2 * h + pair
+                q_copy = keep.tile([P, 2, HALF], F32, name="q_copy%d" % step)
+                low = keep.tile([P, 2, HALF], F32, name="low%d" % step)
+                result = keep.tile([P, 2, HALF], F32, name="result%d" % step)
+                q_banks, p_banks = [], []
+                for i in range(2):
+                    m = 2 * pair + i
+                    q_bank = psum.tile([P, HALF], F32, name="q_bank", tag="q_bank%d" % m)
+                    nc.tensor.matmul_mx(
+                        out=q_bank[:],
+                        lhsT=wb_codes[:, 2 * m * P : 2 * (m + 1) * P].bitcast(FP4X4),
+                        lhsT_scale=wb_plane[:, m * P : (m + 1) * P],
+                        rhs=xb[h][:].bitcast(FP8X4),
+                        rhs_scale=x_planes[h][:, HALF : 2 * HALF],
+                        start=True,
+                        stop=True,
+                    )
+                    nc.scalar.copy(q_copy[:, i, :], q_bank[:])
+                    if step == 1:
+                        quantize(m)
+                    p_bank = psum.tile([P, HALF], F32, name="p_bank%d" % m)
+                    nc.tensor.matmul_mx(
+                        out=p_bank[:],
+                        lhsT=wa_codes[m][:].bitcast(FP8X4),
+                        lhsT_scale=wa_planes[m][:],
+                        rhs=xa[h][:].bitcast(FP8X4),
+                        rhs_scale=x_planes[h][:, 0:HALF],
+                        start=True,
+                        stop=True,
+                    )
+                    q_banks.append(q_bank)
+                    p_banks.append(p_bank)
+                if step == 0:
+                    cast(3)
+                for i in range(2):
+                    nc.vector.tensor_tensor(low[:, i, :], p_banks[i][:], q_copy[:, i, :], ALU.min)
+                rows = out[2 * pair * P : (2 * pair + 2) * P, cols].rearrange("(i p) j -> p i j", p=P)
+                if step == 3:
+                    sums = psum.tile([P, 2, HALF], F32, name="sums", tag="q_bank0")
+                    for i in range(2):
+                        m = 2 * pair + i
+                        for c0 in range(0, HALF, P):
+                            nc.tensor.matmul_mx(
+                                out=sums[:, i, c0 : c0 + P],
+                                lhsT=wb_codes[:, 2 * m * P : 2 * (m + 1) * P].bitcast(FP4X4),
+                                lhsT_scale=wb_plane[:, m * P : (m + 1) * P],
+                                rhs=xb[h][:, c0 : c0 + P].bitcast(FP8X4),
+                                rhs_scale=x_planes[h][:, HALF + c0 : HALF + c0 + P],
+                                start=True,
+                                stop=False,
+                            )
+                            nc.tensor.matmul_mx(
+                                out=sums[:, i, c0 : c0 + P],
+                                lhsT=wa_codes[m][:].bitcast(FP8X4),
+                                lhsT_scale=wa_planes[m][:],
+                                rhs=xa[h][:, c0 : c0 + P].bitcast(FP8X4),
+                                rhs_scale=x_planes[h][:, c0 : c0 + P],
+                                start=False,
+                                stop=True,
+                            )
+                    for i in range(2):
+                        nc.vector.scalar_tensor_tensor(
+                            result[:, i, :], low[:, i, :], -1.3, sums[:, i, :], ALU.mult, ALU.add
+                        )
+                        nc.sync.dma_start(rows[:, i, :], result[:, i, :])
+                    continue
+                part = keep.tile([P, 2, HALF], F32, name="part%d" % step)
+                for i in range(2):
+                    nc.vector.scalar_tensor_tensor(part[:, i, :], low[:, i, :], -1.3, p_banks[i][:], ALU.mult, ALU.add)
+                if step < 2:
+                    nc.gpsimd.tensor_tensor(result[:], part[:], q_copy[:], ALU.add)
+                    nc.sync.dma_start(rows, result[:])
                 else:
-                    nc.vector.tensor_tensor(result[:, cols], q_bank[:, cols], part[:, cols], ALU.add)
-            nc.sync.dma_start(out[m * P : (m + 1) * P, :], result[:])
+                    nc.gpsimd.tensor_tensor(result[:, 0, :], part[:, 0, :], q_copy[:, 0, :], ALU.add)
+                    nc.sync.dma_start(rows[:, 0, :], result[:, 0, :])
+                    nc.vector.tensor_tensor(result[:, 1, :], q_banks[1][:], part[:, 1, :], ALU.add)
+                    nc.sync.dma_start(rows[:, 1, :], result[:, 1, :])

@@ -33,11 +33,14 @@ def tile_moe_expert_heads_twice_kernel(tc, xt_words, xt_scales, wa, wb_words, wb
         word_window = keep.tile([P, T], I32, name="word_window", align_bytes=64)
         wb_plane = keep.tile([P, N], U8, name="wb_plane", align_bytes=64)
         wb_codes = keep.tile([P, 2 * N], U8, name="wb_codes", align_bytes=64)
-        wa_raw = [keep.tile([P, PACK, N // 2], F32, name="wa_raw%d" % h) for h in range(2)]
+        wa_spans = [slice(0, 2 * P), slice(2 * P, 3 * P), slice(3 * P, 4 * P)]
+        wa_raw = [
+            keep.tile([P, PACK, span.stop - span.start], F32, name="wa_raw%d" % i) for i, span in enumerate(wa_spans)
+        ]
         wa_rows = wa.rearrange("(p r) n -> p r n", r=PACK)
 
-        def load_wb_scales(x):
-            nc.sync.dma_start(
+        def load_wb_scales(x, queue):
+            queue.dma_start(
                 wb_plane[32 * x : 32 * x + 32, :].bitcast(I32),
                 wb_scales[0][4 * x : 4 * x + 4, :].bitcast(I32).unsqueeze(0).to_broadcast([8, 4, N // 4]),
             )
@@ -47,13 +50,13 @@ def tile_moe_expert_heads_twice_kernel(tc, xt_words, xt_scales, wa, wb_words, wb
         )
         nc.sync.dma_start(list_b[:], offs2)
         nc.sync.dma_start(list_a[:], offs)
-        nc.sync.dma_start(wa_raw[0][:], wa_rows[:, :, 0 : N // 2])
-        for x in range(3):
-            load_wb_scales(x)
+        nc.sync.dma_start(wa_raw[0][:], wa_rows[:, :, wa_spans[0]])
+        for x in range(4):
+            load_wb_scales(x, nc.sync if x < 2 else nc.gpsimd)
         nc.sync.dma_start(word_window[:], xt_words[0].rearrange("p c r -> p (c r)").bitcast(I32))
-        load_wb_scales(3)
+        nc.sync.dma_start(wa_raw[1][:], wa_rows[:, :, wa_spans[1]])
         nc.sync.dma_start(wb_codes[:].bitcast(I32), wb_words[0].bitcast(I32))
-        nc.sync.dma_start(wa_raw[1][:], wa_rows[:, :, N // 2 : N])
+        nc.sync.dma_start(wa_raw[2][:], wa_rows[:, :, wa_spans[2]])
 
         x_planes = []
         for h in range(2):
@@ -73,8 +76,9 @@ def tile_moe_expert_heads_twice_kernel(tc, xt_words, xt_scales, wa, wb_words, wb
 
         def cast(m):
             g = keep.tile([P, P, PACK], BF16, name="wa_grouped%d" % m, align_bytes=64)
-            c0 = (m % 2) * P
-            nc.scalar.copy(g[:], wa_raw[m // 2][:, :, c0 : c0 + P].rearrange("p r n -> p n r"))
+            piece = max(m - 1, 0)
+            c0 = m * P - wa_spans[piece].start
+            nc.scalar.copy(g[:], wa_raw[piece][:, :, c0 : c0 + P].rearrange("p r n -> p n r"))
             grouped.append(g)
 
         def quantize(m):
@@ -99,7 +103,9 @@ def tile_moe_expert_heads_twice_kernel(tc, xt_words, xt_scales, wa, wb_words, wb
         quantize(0)
         quantize(1)
         gather_words(1)
-        cast(2)
+        for m in (2, 3):
+            cast(m)
+            quantize(m)
 
         for h in range(2):
             cols = slice(h * HALF, (h + 1) * HALF)
@@ -122,8 +128,6 @@ def tile_moe_expert_heads_twice_kernel(tc, xt_words, xt_scales, wa, wb_words, wb
                         stop=True,
                     )
                     nc.scalar.copy(q_copy[:, i, :], q_bank[:])
-                    if step == 1:
-                        quantize(m)
                     p_bank = psum.tile([P, HALF], F32, name="p_bank%d" % m)
                     nc.tensor.matmul_mx(
                         out=p_bank[:],
@@ -136,8 +140,6 @@ def tile_moe_expert_heads_twice_kernel(tc, xt_words, xt_scales, wa, wb_words, wb
                     )
                     q_banks.append(q_bank)
                     p_banks.append(p_bank)
-                if step == 0:
-                    cast(3)
                 for i in range(2):
                     nc.vector.tensor_tensor(low[:, i, :], p_banks[i][:], q_copy[:, i, :], ALU.min)
                 rows = out[2 * pair * P : (2 * pair + 2) * P, cols].rearrange("(i p) j -> p i j", p=P)
@@ -168,7 +170,7 @@ def tile_moe_expert_heads_twice_kernel(tc, xt_words, xt_scales, wa, wb_words, wb
                         nc.vector.scalar_tensor_tensor(
                             result[:, i, :], low[:, i, :], -1.3, sums[:, i, :], ALU.mult, ALU.add
                         )
-                        nc.sync.dma_start(rows[:, i, :], result[:, i, :])
+                        nc.scalar.dma_start(rows[:, i, :], result[:, i, :])
                     continue
                 part = keep.tile([P, 2, HALF], F32, name="part%d" % step)
                 for i in range(2):

from contextlib import ExitStack

import concourse.mybir as mybir

K, T, J, N = 512, 1024, 512, 512
FLOPS = 2 * 2 * K * N * J

F32 = mybir.dt.float32
BF16 = mybir.dt.bfloat16
I32 = mybir.dt.int32
U32 = mybir.dt.uint32
U16 = mybir.dt.uint16
U8 = mybir.dt.uint8
FP8X4 = mybir.dt.float8_e4m3fn_x4
FP4X4 = mybir.dt.float4_e2m1fn_x4
ALU = mybir.AluOpType

P = 128
PACK = 4
TILES = N // P
HALF = J // 2


def tile_moe_expert_heads_twice_kernel(tc, xt_words, xt_scales, wa, wb_words, wb_scales, offs, offs2, out):
    nc = tc.nc
    with ExitStack() as ctx:
        keep = ctx.enter_context(tc.tile_pool(name="keep", bufs=1))
        psum = ctx.enter_context(tc.psum_pool(name="psum", bufs=1))

        list_a = keep.tile([P, J // 16], U16, name="list_a")
        list_b = keep.tile([P, J // 16], U16, name="list_b")
        scale_window = keep.tile([P, T], U8, name="scale_window", align_bytes=64)
        word_window = keep.tile([P, T], I32, name="word_window", align_bytes=64)
        wb_plane = keep.tile([P, N], U8, name="wb_plane", align_bytes=64)
        wb_codes = keep.tile([P, 2 * N], U8, name="wb_codes", align_bytes=64)
        wa_spans = [slice(0, 2 * P), slice(2 * P, 3 * P), slice(3 * P, 4 * P)]
        wa_raw = [
            keep.tile([P, PACK, span.stop - span.start], F32, name="wa_raw%d" % i) for i, span in enumerate(wa_spans)
        ]
        wa_rows = wa.rearrange("(p r) n -> p r n", r=PACK)

        def load_wb_scales(x, queue):
            queue.dma_start(
                wb_plane[32 * x : 32 * x + 32, :].bitcast(I32),
                wb_scales[0][4 * x : 4 * x + 4, :].bitcast(I32).unsqueeze(0).to_broadcast([8, 4, N // 4]),
            )

        nc.sync.dma_start(
            scale_window[:].bitcast(I32), xt_scales[0].bitcast(I32).unsqueeze(1).to_broadcast([16, 8, T // 4])
        )
        nc.sync.dma_start(list_b[:], offs2)
        nc.sync.dma_start(list_a[:], offs)
        nc.sync.dma_start(wa_raw[0][:], wa_rows[:, :, wa_spans[0]])
        for x in range(4):
            load_wb_scales(x, nc.sync if x < 2 else nc.gpsimd)
        nc.sync.dma_start(word_window[:], xt_words[0].rearrange("p c r -> p (c r)").bitcast(I32))
        nc.sync.dma_start(wa_raw[1][:], wa_rows[:, :, wa_spans[1]])
        nc.sync.dma_start(wb_codes[:].bitcast(I32), wb_words[0].bitcast(I32))
        nc.sync.dma_start(wa_raw[2][:], wa_rows[:, :, wa_spans[2]])

        x_planes = []
        for h in range(2):
            entries = slice(h * HALF // 16, (h + 1) * HALF // 16)
            x_plane = keep.tile([P, 2 * HALF], U8, name="x_plane%d" % h, align_bytes=64)
            nc.vector.memset(x_plane[:].bitcast(I32), 0)
            picked = keep.tile([P, 2 * HALF], U8, name="picked_scales%d" % h, align_bytes=64)
            nc.vector.tensor_copy(picked[:, HALF : 2 * HALF], scale_window[:].indirect(list_b[:, entries]))
            nc.vector.tensor_copy(picked[:, 0:HALF], scale_window[:].indirect(list_a[:, entries]))
            for x in range(4):
                nc.sync.dma_start(
                    x_plane[32 * x : 32 * x + 4, :].bitcast(I32), picked[32 * x : 32 * x + 32 : 8, :].bitcast(I32)
                )
            x_planes.append(x_plane)

        wa_codes, wa_planes, grouped, xa, xb = [], [], [], [], []

        def cast(m):
            g = keep.tile([P, P, PACK], BF16, name="wa_grouped%d" % m, align_bytes=64)
            piece = max(m - 1, 0)
            c0 = m * P - wa_spans[piece].start
            nc.scalar.copy(g[:], wa_raw[piece][:, :, c0 : c0 + P].rearrange("p r n -> p n r"))
            grouped.append(g)

        def quantize(m):
            codes = keep.tile([P, P], U32, name="wa_codes%d" % m, align_bytes=64)
            plane = keep.tile([P, P], U8, name="wa_plane%d" % m, align_bytes=64)
            nc.vector.quantize_mx(
                out=codes[:].bitcast(FP8X4), scales=plane[:], in_=grouped[m][:].rearrange("p n r -> p (n r)")
            )
            wa_codes.append(codes)
            wa_planes.append(plane)

        def gather_words(h):
            entries = slice(h * HALF // 16, (h + 1) * HALF // 16)
            for name, offsets, picked in (("xb", list_b, xb), ("xa", list_a, xa)):
                words = keep.tile([P, HALF], U32, name="%s%d" % (name, h), align_bytes=64)
                nc.vector.tensor_copy(words[:], word_window[:].bitcast(U32).indirect(offsets[:, entries]))
                picked.append(words)

        cast(0)
        cast(1)
        gather_words(0)
        quantize(0)
        quantize(1)
        gather_words(1)
        for m in (2, 3):
            cast(m)
            quantize(m)

        for h in range(2):
            cols = slice(h * HALF, (h + 1) * HALF)
            for pair in range(2):
                step = 2 * h + pair
                q_copy = keep.tile([P, 2, HALF], F32, name="q_copy%d" % step)
                low = keep.tile([P, 2, HALF], F32, name="low%d" % step)
                result = keep.tile([P, 2, HALF], F32, name="result%d" % step)
                q_banks, p_banks = [], []
                for i in range(2):
                    m = 2 * pair + i
                    q_bank = psum.tile([P, HALF], F32, name="q_bank", tag="q_bank%d" % m)
                    nc.tensor.matmul_mx(
                        out=q_bank[:],
                        lhsT=wb_codes[:, 2 * m * P : 2 * (m + 1) * P].bitcast(FP4X4),
                        lhsT_scale=wb_plane[:, m * P : (m + 1) * P],
                        rhs=xb[h][:].bitcast(FP8X4),
                        rhs_scale=x_planes[h][:, HALF : 2 * HALF],
                        start=True,
                        stop=True,
                    )
                    nc.scalar.copy(q_copy[:, i, :], q_bank[:])
                    p_bank = psum.tile([P, HALF], F32, name="p_bank%d" % m)
                    nc.tensor.matmul_mx(
                        out=p_bank[:],
                        lhsT=wa_codes[m][:].bitcast(FP8X4),
                        lhsT_scale=wa_planes[m][:],
                        rhs=xa[h][:].bitcast(FP8X4),
                        rhs_scale=x_planes[h][:, 0:HALF],
                        start=True,
                        stop=True,
                    )
                    q_banks.append(q_bank)
                    p_banks.append(p_bank)
                for i in range(2):
                    nc.vector.tensor_tensor(low[:, i, :], p_banks[i][:], q_copy[:, i, :], ALU.min)
                rows = out[2 * pair * P : (2 * pair + 2) * P, cols].rearrange("(i p) j -> p i j", p=P)
                if step == 3:
                    sums = psum.tile([P, 2, HALF], F32, name="sums", tag="q_bank0")
                    for i in range(2):
                        m = 2 * pair + i
                        for c0 in range(0, HALF, P):
                            nc.tensor.matmul_mx(
                                out=sums[:, i, c0 : c0 + P],
                                lhsT=wb_codes[:, 2 * m * P : 2 * (m + 1) * P].bitcast(FP4X4),
                                lhsT_scale=wb_plane[:, m * P : (m + 1) * P],
                                rhs=xb[h][:, c0 : c0 + P].bitcast(FP8X4),
                                rhs_scale=x_planes[h][:, HALF + c0 : HALF + c0 + P],
                                start=True,
                                stop=False,
                            )
                            nc.tensor.matmul_mx(
                                out=sums[:, i, c0 : c0 + P],
                                lhsT=wa_codes[m][:].bitcast(FP8X4),
                                lhsT_scale=wa_planes[m][:],
                                rhs=xa[h][:, c0 : c0 + P].bitcast(FP8X4),
                                rhs_scale=x_planes[h][:, c0 : c0 + P],
                                start=False,
                                stop=True,
                            )
                    for i in range(2):
                        nc.vector.scalar_tensor_tensor(
                            result[:, i, :], low[:, i, :], -1.3, sums[:, i, :], ALU.mult, ALU.add
                        )
                        nc.scalar.dma_start(rows[:, i, :], result[:, i, :])
                    continue
                part = keep.tile([P, 2, HALF], F32, name="part%d" % step)
                for i in range(2):
                    nc.vector.scalar_tensor_tensor(part[:, i, :], low[:, i, :], -1.3, p_banks[i][:], ALU.mult, ALU.add)
                if step < 2:
                    nc.gpsimd.tensor_tensor(result[:], part[:], q_copy[:], ALU.add)
                    nc.sync.dma_start(rows, result[:])
                else:
                    nc.gpsimd.tensor_tensor(result[:, 0, :], part[:, 0, :], q_copy[:, 0, :], ALU.add)
                    nc.sync.dma_start(rows[:, 0, :], result[:, 0, :])
                    nc.vector.tensor_tensor(result[:, 1, :], q_banks[1][:], part[:, 1, :], ALU.add)
                    nc.sync.dma_start(rows[:, 1, :], result[:, 1, :])
